import numpy as np
import ml_dtypes


def mxq(x, axis, fmt="e4m3"):
    dtype, down = {"e4m3": (ml_dtypes.float8_e4m3fn, 7), "e5m2": (ml_dtypes.float8_e5m2, 14)}[fmt]
    v = np.moveaxis(np.asarray(x, np.float32).astype(ml_dtypes.bfloat16).astype(np.float64), axis, -1)
    blocks = v.reshape(v.shape[:-1] + (-1, 32))
    amax = np.abs(blocks).max(-1, keepdims=True)
    byte = np.maximum(np.where(amax > 0, np.frexp(amax)[1] - 1 + 127, 0) - down, 1)
    scale = np.exp2(byte - 127.0)
    codes = (blocks / scale).astype(np.float32).astype(dtype).astype(np.float64)
    return np.moveaxis((codes * scale).reshape(v.shape), -1, axis)


WIDE = False


def mx_kscale(k):
    if not WIDE:
        return np.ones(k)
    levels = np.array([10, -10, 5, -5, 0])
    if k % 512:
        return np.exp2(np.random.permutation(np.resize(levels, k // 32))).repeat(32)
    a = np.empty((k // 512, 16))
    for p in range(k // 512):
        a[p, :8] = np.random.permutation(np.resize(levels, 8))
        for g in range(8):
            far = levels[np.abs(levels - a[p, g]) >= 10]
            a[p, g + 8] = far[np.random.randint(len(far))]
    return np.exp2(a.ravel()).repeat(32)


def f64(x):
    return np.asarray(x).astype(np.float64)


def striped(idx):
    return np.tile(idx.reshape(-1, 16).T, (8, 1)).astype(np.uint16)


def unstriped(offs):
    return offs[:16].T.reshape(-1).astype(np.int64)


K, T, D, S, V, N = 512, 1024, 2, 1024, 512, 512


def setup_inputs():
    n = np.random.standard_normal
    s = mx_kscale(K)[:, None]
    return {
        "xT": (n((K, T)) * s / np.sqrt(D)).astype(ml_dtypes.bfloat16).astype(np.float32),
        "w": (n((K, N)) / np.sqrt(K) / s).astype(np.float32),
        "b": (0.3 * n((N, 1))).astype(np.float32),
        "offs": striped(np.concatenate([np.random.permutation(T)[:V] for _ in range(D)])),
    }


def reference(xT, w, b, offs):
    idx = unstriped(offs)
    x = sum(f64(xT)[:, idx[d * V:(d + 1) * V]] for d in range(D))
    return (mxq(f64(w), 0, "e4m3").T @ mxq(x, 0, "e4m3")) + f64(b)

from contextlib import ExitStack

import concourse.mybir as mybir
from concourse.masks import make_identity

K, T, D, V, N = 512, 1024, 2, 512, 512
FLOPS = 2 * K * N * V

F32 = mybir.dt.float32
BF16 = mybir.dt.bfloat16
U32 = mybir.dt.uint32
U16 = mybir.dt.uint16
U8 = mybir.dt.uint8
FP8X4 = mybir.dt.float8_e4m3fn_x4
ADD = mybir.AluOpType.add
MULT = mybir.AluOpType.mult
IDENT = mybir.ActivationFunctionType.Identity

P = 128
PACK = 4
LANES = 16
M_BLOCKS = N // P

X_LOADS = (
    ((0, 512, ((0, 512, "v"),)), (512, 768, ((512, 768, "v"),)), (768, 1024, ((768, 1024, "v"),))),
    ((0, 256, ((0, 256, "s"),)), (256, 512, ((256, 512, "s"),)), (512, 768, ((512, 768, "s"),)), (768, 1024, ((768, 1024, "s"),))),
)
W_LOADS = ((0, 256, ((0, 128, "s"), (128, 256, "s"))), (256, 512, ((256, 512, "s"),)))
PIECES = (
    (0, 256, ((0, 2, "s"), (2, 4, "s"))),
    (256, 384, ((0, 2, "s"), (2, 4, "v"))),
    (384, 512, ((0, 2, "s"), (2, 4, "v"))),
)


def tile_picked_hash_lin_bias_sub_l_kernel(tc, xT, w, b, offs, out):
    nc = tc.nc
    x_rows = xT.rearrange("(p u e) t -> p u e t", u=2, e=2)
    w_rows = w.rearrange("(p j) m -> p j m", j=PACK)
    out_rows = out.rearrange("(c p) v -> p c v", p=P)

    def cast(eng, dst, src):
        if eng == "v":
            nc.vector.tensor_copy(out=dst, in_=src)
        elif eng == "s":
            nc.scalar.copy(out=dst, in_=src)
        else:
            nc.gpsimd.tensor_scalar(out=dst, in0=src, scalar1=1.0, scalar2=0.0, op0=MULT, op1=ADD)

    with ExitStack() as ctx:
        keep = ctx.enter_context(tc.tile_pool(name="keep", bufs=1))
        psum = ctx.enter_context(tc.psum_pool(name="psum", bufs=1))

        offsets = keep.tile([P, D * V // LANES], U16, name="offsets")
        bias = keep.tile([P, M_BLOCKS], F32, name="bias")
        warm_in = keep.tile([P, 8], F32, name="warm_in")
        warm_out = keep.tile([P, 8], F32, name="warm_out")
        nc.gpsimd.memset(warm_in[:], 0.0)
        nc.scalar.activation(out=warm_out[:], in_=warm_in[:], func=IDENT)

        x_raw = {}
        first = True
        for u in range(2):
            for c0, c1, shares in X_LOADS[u]:
                x_raw[u, c0] = keep.tile([P, 2, c1 - c0], F32, name=f"x_raw{u}_{c0}")
                nc.sync.dma_start(out=x_raw[u, c0][:], in_=x_rows[:, u, :, c0:c1])
                if first:
                    nc.sync.dma_start(offsets[:], offs)
                    first = False
        w_raw = {}
        for c0, c1, shares in W_LOADS:
            w_raw[c0] = keep.tile([P, PACK, c1 - c0], F32, name=f"w_raw{c0}")
            nc.sync.dma_start(out=w_raw[c0][:], in_=w_rows[:, :, c0:c1])
        with nc.allow_non_contiguous_dma(reason="one bias value a partition"):
            nc.sync.dma_start(out=bias[:], in_=b.rearrange("(c p) o -> p (c o)", p=P))

        pairs = [keep.tile([P, T, 2], BF16, name=f"pairs{u}") for u in range(2)]
        picked0 = keep.tile([P, 2, V, 2], BF16, name="picked0")
        shared = keep.tile([P, 3 * V + (N - P) * PACK], BF16, name="shared", align_bytes=64)
        picked = [picked0[:], shared[:, : 4 * V].rearrange("p (u v e) -> p u v e", u=2, e=2)]

        def pair_up(u):
            for c0, c1, shares in X_LOADS[u]:
                for s0, s1, eng in shares:
                    cast(eng, pairs[u][:, s0:s1, :], x_raw[u, c0][:, :, s0 - c0 : s1 - c0].rearrange("p e t -> p t e"))

        def gather(u, d, v0, v1):
            window = pairs[u][:].rearrange("p t e -> p (t e)").bitcast(U32)
            dst = picked[d][:, u, v0:v1, :].rearrange("p v e -> p (v e)").bitcast(U32)
            o0 = (d * V + v0) // LANES
            nc.vector.tensor_copy(out=dst, in_=window.indirect(offsets[:, o0 : o0 + (v1 - v0) // LANES]))

        w_first = keep.tile([P, P, PACK], BF16, name="w_first", align_bytes=64)
        w_rest = shared[:, 3 * V :].rearrange("p (m j) -> p m j", j=PACK)

        def w_bf(c0, c1):
            return w_first[:, c0:c1, :] if c1 <= P else w_rest[:, c0 - P : c1 - P, :]

        w_codes = keep.tile([P, N], U32, name="w_codes", align_bytes=64)
        w_scales = keep.tile([P, N], U8, name="w_scales", align_bytes=64)

        def cast_w():
            for c0, c1, shares in W_LOADS:
                for s0, s1, eng in shares:
                    cast(
                        eng,
                        w_bf(s0, s1).rearrange("p (c i) j -> p c j i", i=4),
                        w_raw[c0][:, :, s0 - c0 : s1 - c0].rearrange("p j (c i) -> p c j i", i=4),
                    )

        def quantize_w(c0, c1):
            nc.vector.quantize_mx(
                out=w_codes[:, c0:c1].bitcast(FP8X4),
                scales=w_scales[:, c0:c1],
                in_=w_bf(c0, c1).rearrange("p m j -> p (m j)"),
            )

        identity = keep.tile([P, P], BF16, name="identity")
        make_identity(nc, identity[:])
        idle = [psum.tile([P, 8, P], BF16, name=f"idle{h}") for h in range(2)]

        def warm_tensor(count):
            source = pairs[1][:].rearrange("p t e -> p (t e)")[:, T:]
            for i in range(count):
                nc.tensor.transpose(idle[i // 8 % 2][:, i % 8, :], source[:, (i % 8) * P : (i % 8 + 1) * P], identity[:])

        x_bf, x_codes, x_scales = {}, {}, {}

        def add(i):
            v0, v1, groups = PIECES[i]
            x_bf[i] = keep.tile([P, v1 - v0, 2, 2], BF16, name=f"x_bf{i}", align_bytes=64)
            nc.vector.tensor_tensor(
                out=x_bf[i][:],
                in0=picked[0][:, :, v0:v1, :].rearrange("p u v e -> p v u e"),
                in1=picked[1][:, :, v0:v1, :].rearrange("p u v e -> p v u e"),
                op=ADD,
            )

        def quantize_x(i):
            v0, v1, groups = PIECES[i]
            x_codes[i] = keep.tile([P, v1 - v0], U32, name=f"x_codes{i}", align_bytes=64)
            x_scales[i] = keep.tile([P, v1 - v0], U8, name=f"x_scales{i}", align_bytes=64)
            nc.vector.quantize_mx(
                out=x_codes[i][:].bitcast(FP8X4),
                scales=x_scales[i][:],
                in_=x_bf[i][:].rearrange("p v u e -> p (v u e)"),
            )

        def multiply(i):
            v0, v1, groups = PIECES[i]
            n = v1 - v0
            banks = []
            for g, (c0, c1, eng) in enumerate(groups):
                bank = psum.tile([P, c1 - c0, n], F32, name=f"bank{i}_{g}")
                banks.append(bank)
                for c in range(c0, c1):
                    nc.tensor.matmul_mx(
                        out=bank[:, c - c0, :],
                        lhsT=w_codes[:, c * P : (c + 1) * P].bitcast(FP8X4),
                        lhsT_scale=w_scales[:, c * P : (c + 1) * P],
                        rhs=x_codes[i][:].bitcast(FP8X4),
                        rhs_scale=x_scales[i][:],
                        start=True,
                        stop=True,
                    )
            return banks

        def leave(i, banks):
            v0, v1, groups = PIECES[i]
            n = v1 - v0
            for g, (c0, c1, eng) in enumerate(groups):
                result = keep.tile([P, c1 - c0, n], F32, name=f"result{i}_{g}")
                for c in range(c0, c1):
                    if eng == "s":
                        nc.scalar.activation(
                            out=result[:, c - c0, :], in_=banks[g][:, c - c0, :], func=IDENT, bias=bias[:, c : c + 1]
                        )
                    else:
                        nc.vector.tensor_scalar(
                            out=result[:, c - c0, :],
                            in0=banks[g][:, c - c0, :],
                            scalar1=bias[:, c : c + 1],
                            scalar2=None,
                            op0=ADD,
                        )
                nc.sync.dma_start(out=out_rows[:, c0:c1, v0:v1], in_=result[:])

        pair_up(0)
        pair_up(1)
        cast_w()
        warm_tensor(20)
        gather(0, 0, 0, V)
        gather(0, 1, 0, V)
        gather(1, 0, 0, 256)
        gather(1, 1, 0, 256)
        gather(1, 0, 256, 384)
        add(0)
        gather(1, 0, 384, 512)
        quantize_x(0)
        quantize_w(0, 128)
        quantize_w(128, 384)
        quantize_w(384, 512)
        banks0 = multiply(0)
        gather(1, 1, 256, 384)
        gather(1, 1, 384, 512)
        add(1)
        add(2)
        quantize_x(1)
        quantize_x(2)
        banks1 = multiply(1)
        banks2 = multiply(2)
        leave(0, banks0)
        leave(1, banks1)
        leave(2, banks2)
